import numpy as np
import ml_dtypes


def mxq(x, axis, fmt="e4m3"):
    dtype, down = {"e4m3": (ml_dtypes.float8_e4m3fn, 7), "e5m2": (ml_dtypes.float8_e5m2, 14)}[fmt]
    v = np.moveaxis(np.asarray(x, np.float32).astype(ml_dtypes.bfloat16).astype(np.float64), axis, -1)
    blocks = v.reshape(v.shape[:-1] + (-1, 32))
    amax = np.abs(blocks).max(-1, keepdims=True)
    byte = np.maximum(np.where(amax > 0, np.frexp(amax)[1] - 1 + 127, 0) - down, 1)
    scale = np.exp2(byte - 127.0)
    codes = (blocks / scale).astype(np.float32).astype(dtype).astype(np.float64)
    return np.moveaxis((codes * scale).reshape(v.shape), -1, axis)


WIDE = False


def mx_kscale(k):
    if not WIDE:
        return np.ones(k)
    levels = np.array([10, -10, 5, -5, 0])
    if k % 512:
        return np.exp2(np.random.permutation(np.resize(levels, k // 32))).repeat(32)
    a = np.empty((k // 512, 16))
    for p in range(k // 512):
        a[p, :8] = np.random.permutation(np.resize(levels, 8))
        for g in range(8):
            far = levels[np.abs(levels - a[p, g]) >= 10]
            a[p, g + 8] = far[np.random.randint(len(far))]
    return np.exp2(a.ravel()).repeat(32)


def f64(x):
    return np.asarray(x).astype(np.float64)


def striped8(idx):
    return np.asarray(idx).reshape(8, -1, 16).transpose(0, 2, 1).reshape(128, -1).astype(np.uint16)


def unstriped8(offs):
    return offs.reshape(8, 16, -1).transpose(0, 2, 1).reshape(8, -1).astype(np.int64)


def pick8(x, idx, run):
    r = np.arange(len(x))
    return x[r[:, None], idx[r % (8 * run) // run]]


E2M1 = np.array([0.0, 0.5, 1.0, 1.5, 2.0, 3.0, 4.0, 6.0, -0.0, -0.5, -1.0, -1.5, -2.0, -3.0, -4.0, -6.0])


def pack_weight(w, fmt):
    k, n = w.shape
    w = f64(np.asarray(w, np.float32).astype(ml_dtypes.bfloat16)).reshape(k // 32, 32, n)
    amax = np.abs(w).max(1)
    if fmt == "e4m3":
        byte = np.frexp(amax)[1] - 1 + 127 - 7
    else:
        mant, ex = np.frexp(amax / 6.0)
        byte = np.where(mant > 0.5, ex, ex - 1) + 127
    byte = np.clip(np.where(amax > 0, byte, 1), 1, 254)
    scaled = (w * np.exp2(127.0 - byte)[:, None, :]).reshape(k, n).astype(np.float32)
    by_word = np.ascontiguousarray(scaled.reshape(k // 512, 128, 4, n).transpose(0, 1, 3, 2))
    if fmt == "e4m3":
        words = by_word.astype(ml_dtypes.float8_e4m3fn).view(np.uint8)
    else:
        c = by_word.astype(ml_dtypes.float4_e2m1fn).view(np.uint8) & 0xF
        words = (c[..., 0::2] | (c[..., 1::2] << 4)).reshape(k // 512, 128, 2 * n)
    return np.ascontiguousarray(words), np.ascontiguousarray(byte.astype(np.uint8).reshape(k // 512, 16, n))


def unpack_weight(words, scales, fmt):
    g, _, n = scales.shape
    words = np.ascontiguousarray(words).reshape(g, 128, n, -1)
    if fmt == "e4m3":
        vals = words.view(ml_dtypes.float8_e4m3fn).astype(np.float64)
    else:
        nib = np.empty((g, 128, n, 4), np.uint8)
        nib[..., 0::2] = words & 0xF
        nib[..., 1::2] = words >> 4
        vals = E2M1[nib]
    vals = vals * np.repeat(np.exp2(scales.astype(np.float64) - 127.0), 8, axis=1)[..., None]
    return vals.transpose(0, 1, 3, 2).reshape(g * 512, n)


D, T, I, Q = 512, 1024, 512, 128


def setup_inputs():
    n = np.random.standard_normal
    idx = np.stack([np.random.permutation(T)[:I] for _ in range(8)])
    idx2 = np.stack([np.random.permutation(T)[:I] for _ in range(8)])
    idx3 = np.stack([np.random.permutation(T)[:I] for _ in range(8)])
    fd = mx_kscale(D)
    keysp = pack_weight(n((D, T)) / fd[:, None], "e4m3")
    return {
        "query": (n((D, Q)) * 1.2 / np.sqrt(D) * fd[:, None]).astype(np.float32),
        "keys_words": keysp[0],
        "keys_scales": keysp[1],
        "lam": (np.random.uniform(0.8, 1.8, (Q, 1))).astype(np.float32),
        "lean": (np.random.uniform(0.2, 0.6, (Q, 1))).astype(np.float32),
        "base": (0.3 * n((Q, I))).astype(np.float32),
        "gain2": (np.random.uniform(0.5, 2.0, (Q, 1))).astype(np.float32),
        "offs": striped8(idx),
        "offs2": striped8(idx2),
        "offs3": striped8(idx3),
    }


def reference(query, keys_words, keys_scales, lam, lean, base, gain2, offs, offs2, offs3):
    idx = unstriped8(offs)
    idx2 = unstriped8(offs2)
    idx3 = unstriped8(offs3)
    keysu = unpack_weight(keys_words, keys_scales, "e4m3")
    queryq = mxq(f64(query), 0, "e4m3")
    a = queryq.T @ keysu
    lo2 = np.minimum(pick8(a, idx, 16), pick8(a, idx2, 16))
    hi2 = np.maximum(pick8(a, idx, 16), pick8(a, idx2, 16))
    s = np.maximum(lo2, np.minimum(hi2, pick8(a, idx3, 16))) * f64(lam)
    p = np.exp(s - np.max(s, axis=1, keepdims=True))
    r = p / np.sum(p, axis=1, keepdims=True)
    m0 = np.sum(r * s, axis=1, keepdims=True)
    w = r * ((s - m0) * f64(lean) + 1.0)
    y = np.tanh(w * f64(gain2) * 128.0) + f64(base)
    return y

@@ -1,0 +1,170 @@
+from contextlib import ExitStack
+
+import concourse.mybir as mybir
+
+D, T, I, Q = 512, 1024, 512, 128
+FLOPS = 2 * D * T * Q
+
+F32 = mybir.dt.float32
+BF16 = mybir.dt.bfloat16
+I32 = mybir.dt.int32
+U32 = mybir.dt.uint32
+U16 = mybir.dt.uint16
+U8 = mybir.dt.uint8
+FP8X4 = mybir.dt.float8_e4m3fn_x4
+ALU = mybir.AluOpType
+ACT = mybir.ActivationFunctionType
+
+P = 128
+PACK = 4
+QUADRANTS = 4
+PASS_N = 256
+PASSES = T // PASS_N
+WORD_LOADS = 2
+WORD_COLS = T // WORD_LOADS
+HALVES = 2
+QUARTERS = 2
+H = I // HALVES
+LIST_COLS = H // 16
+
+
+def tile_attend_middle_leaning_gated_heads_kernel(
+    tc, query, keys_words, keys_scales, lam, lean, base, gain2, offs, offs2, offs3, out
+):
+    nc = tc.nc
+    with ExitStack() as ctx:
+        sb = ctx.enter_context(tc.tile_pool(name="sb", bufs=1))
+        psum = ctx.enter_context(tc.psum_pool(name="psum", bufs=1))
+
+        q_raw = sb.tile([P, PACK, Q], F32, name="q_raw")
+        nc.sync.dma_start(out=q_raw[:], in_=query.rearrange("(p j) q -> p j q", j=PACK))
+
+        k_scales = sb.tile([P, T], U8, name="k_scales", align_bytes=64)
+        for quad in range(QUADRANTS):
+            (nc.sync if quad % 2 else nc.scalar).dma_start(
+                out=k_scales[32 * quad : 32 * quad + 4, :].bitcast(I32),
+                in_=keys_scales[0, 4 * quad : 4 * quad + 4, :].bitcast(I32),
+            )
+        words_in_hbm = keys_words[0].rearrange("p n t -> p (n t)").bitcast(I32)
+        k_words = []
+        for part in range(WORD_LOADS):
+            words = sb.tile([P, WORD_COLS], U32, name="k_words%d" % part, align_bytes=64)
+            nc.sync.dma_start(
+                out=words[:].bitcast(I32), in_=words_in_hbm[:, part * WORD_COLS : (part + 1) * WORD_COLS]
+            )
+            k_words.append(words)
+
+        lists = []
+        for n, src in enumerate((offs, offs2, offs3)):
+            lst = sb.tile([P, I // 16], U16, name="list%d" % n)
+            nc.sync.dma_start(lst[:], src)
+            lists.append(lst)
+
+        lam_t = sb.tile([P, 1], F32, name="lam_t")
+        lean_t = sb.tile([P, 1], F32, name="lean_t")
+        gain_t = sb.tile([P, 1], F32, name="gain_t")
+        base_t = sb.tile([P, I], F32, name="base_t")
+        nc.sync.dma_start(out=lam_t[:], in_=lam)
+        nc.sync.dma_start(out=lean_t[:], in_=lean)
+        nc.sync.dma_start(out=gain_t[:], in_=gain2)
+        nc.sync.dma_start(out=base_t[:], in_=base)
+
+        neg_lam = sb.tile([P, 1], F32, name="neg_lam")
+        nc.gpsimd.tensor_scalar(neg_lam[:], lam_t[:], -1.0, 0.0, ALU.mult, ALU.add)
+
+        q_bf = sb.tile([P, Q, PACK], BF16, name="q_bf", align_bytes=64)
+        nc.vector.tensor_copy(out=q_bf[:], in_=q_raw[:].rearrange("p j q -> p q j"))
+        q_words = sb.tile([P, Q], U32, name="q_words", align_bytes=64)
+        q_scales = sb.tile([P, Q], U8, name="q_scales", align_bytes=64)
+        nc.vector.quantize_mx(
+            out=q_words[:].bitcast(FP8X4),
+            scales=q_scales[:],
+            in_=q_bf[:].rearrange("p q j -> p (q j)"),
+        )
+
+        a = sb.tile([P, T], F32, name="a")
+        for n in range(PASSES):
+            cols = slice(n * PASS_N, (n + 1) * PASS_N)
+            part, at = divmod(n * PASS_N, WORD_COLS)
+            bank = psum.tile([P, PASS_N], F32, name="bank%d" % n)
+            nc.tensor.matmul_mx(
+                out=bank[:],
+                lhsT=q_words[:].bitcast(FP8X4),
+                lhsT_scale=q_scales[:],
+                rhs=k_words[part][:, at : at + PASS_N].bitcast(FP8X4),
+                rhs_scale=k_scales[:, cols],
+                start=True,
+                stop=True,
+            )
+            if n % 2 == 0:
+                nc.vector.tensor_copy(out=a[:, cols], in_=bank[:])
+            else:
+                nc.scalar.copy(out=a[:, cols], in_=bank[:])
+
+        def halves(name, width=H):
+            return [sb.tile([P, width], F32, name="%s%d" % (name, h)) for h in range(HALVES)]
+
+        def looked_up(n, h):
+            return a[:].indirect(lists[n][:, h * LIST_COLS : (h + 1) * LIST_COLS])
+
+        first, second, third = halves("first"), halves("second"), halves("third")
+        for h in range(HALVES):
+            nc.vector.tensor_copy(first[h][:], looked_up(0, h))
+            nc.scalar.activation(second[h][:], looked_up(1, h), ACT.Copy)
+        for h in range(HALVES):
+            nc.scalar.activation(third[h][:], looked_up(2, h), ACT.Copy)
+
+        hi, lo, cap, mid, neg_s = halves("hi"), halves("lo"), halves("cap"), halves("mid"), halves("neg_s")
+        neg_max = halves("neg_max", 1)
+        for h in range(HALVES):
+            nc.vector.tensor_tensor(hi[h][:], first[h][:], second[h][:], ALU.max)
+        for h in range(HALVES):
+            nc.vector.tensor_tensor(lo[h][:], first[h][:], second[h][:], ALU.min)
+            nc.vector.tensor_tensor(cap[h][:], hi[h][:], third[h][:], ALU.min)
+        for h in range(HALVES):
+            nc.vector.tensor_tensor(mid[h][:], lo[h][:], cap[h][:], ALU.max)
+        for h in range(HALVES):
+            start = neg_max[h - 1][:] if h else None
+            nc.vector.tensor_scalar(
+                neg_s[h][:], mid[h][:], neg_lam[:], start, ALU.mult, ALU.min, accum_out=neg_max[h][:]
+            )
+
+        p, lean_ps = halves("p"), halves("lean_ps")
+        p_sum, lean_sum = halves("p_sum", 1), halves("lean_sum", 1)
+        for h in range(HALVES):
+            nc.scalar.activation(
+                p[h][:], neg_s[h][:], ACT.Exp, bias=neg_max[HALVES - 1][:], scale=-1.0, accum_out=p_sum[h][:]
+            )
+
+        z = sb.tile([P, 1], F32, name="z")
+        inv_z = sb.tile([P, 1], F32, name="inv_z")
+        partial = sb.tile([P, 1], F32, name="partial")
+        c = sb.tile([P, 1], F32, name="c")
+        tanh_scale = sb.tile([P, 1], F32, name="tanh_scale")
+
+        def lean_product(h):
+            nc.vector.scalar_tensor_tensor(
+                lean_ps[h][:], neg_s[h][:], lean_t[:], p[h][:], ALU.mult, ALU.mult, accum_out=lean_sum[h][:]
+            )
+
+        lean_product(0)
+        nc.vector.tensor_tensor(z[:], p_sum[0][:], p_sum[1][:], ALU.add)
+        lean_product(1)
+        nc.vector.reciprocal(inv_z[:], z[:])
+        nc.vector.tensor_tensor(partial[:], z[:], lean_sum[0][:], ALU.add)
+        nc.vector.tensor_scalar(c[:], lean_sum[1][:], partial[:], inv_z[:], ALU.add, ALU.mult)
+        nc.vector.tensor_scalar(tanh_scale[:], inv_z[:], gain_t[:], 128.0, ALU.mult, ALU.mult)
+
+        zw, gate, y = halves("zw"), halves("gate"), halves("y")
+        width = H // QUARTERS
+        pieces = [(h, slice(k * width, (k + 1) * width)) for h in range(HALVES) for k in range(QUARTERS)]
+        for h, cols in pieces:
+            nc.vector.scalar_tensor_tensor(
+                zw[h][:, cols], p[h][:, cols], c[:], lean_ps[h][:, cols], ALU.mult, ALU.subtract
+            )
+            nc.scalar.activation(gate[h][:, cols], zw[h][:, cols], ACT.Tanh, scale=tanh_scale[:])
+        for h, cols in pieces:
+            whole = slice(h * H + cols.start, h * H + cols.stop)
+            nc.vector.tensor_tensor(y[h][:, cols], gate[h][:, cols], base_t[:, whole], ALU.add)
+            if cols.stop == H:
+                nc.sync.dma_start(out=out[:, h * H : (h + 1) * H], in_=y[h][:])

@@ -18,12 +18,11 @@ ACT = mybir.ActivationFunctionType
 P = 128
 PACK = 4
 QUADRANTS = 4
-PASS_N = 256
-PASSES = T // PASS_N
+PASS_WIDTHS = (256, 256, 256, 128, 128)
 WORD_LOADS = 2
 WORD_COLS = T // WORD_LOADS
 HALVES = 2
-QUARTERS = 2
+PIECE = 128
 H = I // HALVES
 LIST_COLS = H // 16
 
@@ -72,6 +71,9 @@ def tile_attend_middle_leaning_gated_heads_kernel(
         neg_lam = sb.tile([P, 1], F32, name="neg_lam")
         nc.gpsimd.tensor_scalar(neg_lam[:], lam_t[:], -1.0, 0.0, ALU.mult, ALU.add)
 
+        gain_128 = sb.tile([P, 1], F32, name="gain_128")
+        nc.gpsimd.tensor_scalar(gain_128[:], gain_t[:], 128.0, 0.0, ALU.mult, ALU.add)
+
         q_bf = sb.tile([P, Q, PACK], BF16, name="q_bf", align_bytes=64)
         nc.vector.tensor_copy(out=q_bf[:], in_=q_raw[:].rearrange("p j q -> p q j"))
         q_words = sb.tile([P, Q], U32, name="q_words", align_bytes=64)
@@ -83,15 +85,16 @@ def tile_attend_middle_leaning_gated_heads_kernel(
         )
 
         a = sb.tile([P, T], F32, name="a")
-        for n in range(PASSES):
-            cols = slice(n * PASS_N, (n + 1) * PASS_N)
-            part, at = divmod(n * PASS_N, WORD_COLS)
-            bank = psum.tile([P, PASS_N], F32, name="bank%d" % n)
+        for n, width in enumerate(PASS_WIDTHS):
+            begin = sum(PASS_WIDTHS[:n])
+            cols = slice(begin, begin + width)
+            part, at = divmod(begin, WORD_COLS)
+            bank = psum.tile([P, width], F32, name="bank%d" % n)
             nc.tensor.matmul_mx(
                 out=bank[:],
                 lhsT=q_words[:].bitcast(FP8X4),
                 lhsT_scale=q_scales[:],
-                rhs=k_words[part][:, at : at + PASS_N].bitcast(FP8X4),
+                rhs=k_words[part][:, at : at + width].bitcast(FP8X4),
                 rhs_scale=k_scales[:, cols],
                 start=True,
                 stop=True,
@@ -101,70 +104,68 @@ def tile_attend_middle_leaning_gated_heads_kernel(
             else:
                 nc.scalar.copy(out=a[:, cols], in_=bank[:])
 
-        def halves(name, width=H):
-            return [sb.tile([P, width], F32, name="%s%d" % (name, h)) for h in range(HALVES)]
+        def wide(name):
+            return sb.tile([P, I], F32, name=name)
+
+        def column(name):
+            return sb.tile([P, 1], F32, name=name)
+
+        def half(h):
+            return slice(h * H, (h + 1) * H)
 
         def looked_up(n, h):
             return a[:].indirect(lists[n][:, h * LIST_COLS : (h + 1) * LIST_COLS])
 
-        first, second, third = halves("first"), halves("second"), halves("third")
+        first, second, third = wide("first"), wide("second"), wide("third")
         for h in range(HALVES):
-            nc.vector.tensor_copy(first[h][:], looked_up(0, h))
-            nc.scalar.activation(second[h][:], looked_up(1, h), ACT.Copy)
+            nc.vector.tensor_copy(first[:, half(h)], looked_up(0, h))
+            nc.scalar.activation(second[:, half(h)], looked_up(1, h), ACT.Copy)
         for h in range(HALVES):
-            nc.scalar.activation(third[h][:], looked_up(2, h), ACT.Copy)
+            nc.scalar.activation(third[:, half(h)], looked_up(2, h), ACT.Copy)
 
-        hi, lo, cap, mid, neg_s = halves("hi"), halves("lo"), halves("cap"), halves("mid"), halves("neg_s")
-        neg_max = halves("neg_max", 1)
+        hi, lo, cap, mid, neg_s = wide("hi"), wide("lo"), wide("cap"), wide("mid"), wide("neg_s")
         for h in range(HALVES):
-            nc.vector.tensor_tensor(hi[h][:], first[h][:], second[h][:], ALU.max)
+            nc.vector.tensor_tensor(hi[:, half(h)], first[:, half(h)], second[:, half(h)], ALU.max)
+        nc.vector.tensor_tensor(lo[:], first[:], second[:], ALU.min)
         for h in range(HALVES):
-            nc.vector.tensor_tensor(lo[h][:], first[h][:], second[h][:], ALU.min)
-            nc.vector.tensor_tensor(cap[h][:], hi[h][:], third[h][:], ALU.min)
+            nc.vector.tensor_tensor(cap[:, half(h)], hi[:, half(h)], third[:, half(h)], ALU.min)
         for h in range(HALVES):
-            nc.vector.tensor_tensor(mid[h][:], lo[h][:], cap[h][:], ALU.max)
-        for h in range(HALVES):
-            start = neg_max[h - 1][:] if h else None
-            nc.vector.tensor_scalar(
-                neg_s[h][:], mid[h][:], neg_lam[:], start, ALU.mult, ALU.min, accum_out=neg_max[h][:]
-            )
+            nc.vector.tensor_tensor(mid[:, half(h)], lo[:, half(h)], cap[:, half(h)], ALU.max)
+        neg_max = column("neg_max")
+        nc.vector.tensor_scalar(neg_s[:], mid[:], neg_lam[:], None, ALU.mult, ALU.min, accum_out=neg_max[:])
 
-        p, lean_ps = halves("p"), halves("lean_ps")
-        p_sum, lean_sum = halves("p_sum", 1), halves("lean_sum", 1)
+        p, lean_ps = wide("p"), wide("lean_ps")
+        p_sum = [column("p_sum%d" % h) for h in range(HALVES)]
+        lean_sum = [column("lean_sum%d" % h) for h in range(HALVES)]
         for h in range(HALVES):
             nc.scalar.activation(
-                p[h][:], neg_s[h][:], ACT.Exp, bias=neg_max[HALVES - 1][:], scale=-1.0, accum_out=p_sum[h][:]
+                p[:, half(h)], neg_s[:, half(h)], ACT.Exp, bias=neg_max[:], scale=-1.0, accum_out=p_sum[h][:]
             )
-
-        z = sb.tile([P, 1], F32, name="z")
-        inv_z = sb.tile([P, 1], F32, name="inv_z")
-        partial = sb.tile([P, 1], F32, name="partial")
-        c = sb.tile([P, 1], F32, name="c")
-        tanh_scale = sb.tile([P, 1], F32, name="tanh_scale")
-
-        def lean_product(h):
+        for h in range(HALVES):
             nc.vector.scalar_tensor_tensor(
-                lean_ps[h][:], neg_s[h][:], lean_t[:], p[h][:], ALU.mult, ALU.mult, accum_out=lean_sum[h][:]
+                lean_ps[:, half(h)],
+                neg_s[:, half(h)],
+                lean_t[:],
+                p[:, half(h)],
+                ALU.mult,
+                ALU.mult,
+                accum_out=lean_sum[h][:],
             )
 
-        lean_product(0)
-        nc.vector.tensor_tensor(z[:], p_sum[0][:], p_sum[1][:], ALU.add)
-        lean_product(1)
+        z, inv_z, partial, c, tanh_scale = (column(n) for n in ("z", "inv_z", "partial", "c", "tanh_scale"))
+        nc.scalar.activation(z[:], p_sum[0][:], ACT.Identity, bias=p_sum[1][:])
         nc.vector.reciprocal(inv_z[:], z[:])
-        nc.vector.tensor_tensor(partial[:], z[:], lean_sum[0][:], ALU.add)
+        nc.vector.tensor_scalar(partial[:], lean_sum[0][:], p_sum[0][:], p_sum[1][:], ALU.add, ALU.add)
         nc.vector.tensor_scalar(c[:], lean_sum[1][:], partial[:], inv_z[:], ALU.add, ALU.mult)
-        nc.vector.tensor_scalar(tanh_scale[:], inv_z[:], gain_t[:], 128.0, ALU.mult, ALU.mult)
+        nc.scalar.activation(tanh_scale[:], inv_z[:], ACT.Copy, scale=gain_128[:])
 
-        zw, gate, y = halves("zw"), halves("gate"), halves("y")
-        width = H // QUARTERS
-        pieces = [(h, slice(k * width, (k + 1) * width)) for h in range(HALVES) for k in range(QUARTERS)]
-        for h, cols in pieces:
-            nc.vector.scalar_tensor_tensor(
-                zw[h][:, cols], p[h][:, cols], c[:], lean_ps[h][:, cols], ALU.mult, ALU.subtract
-            )
-            nc.scalar.activation(gate[h][:, cols], zw[h][:, cols], ACT.Tanh, scale=tanh_scale[:])
-        for h, cols in pieces:
-            whole = slice(h * H + cols.start, h * H + cols.stop)
-            nc.vector.tensor_tensor(y[h][:, cols], gate[h][:, cols], base_t[:, whole], ALU.add)
-            if cols.stop == H:
-                nc.sync.dma_start(out=out[:, h * H : (h + 1) * H], in_=y[h][:])
+        zw, gate, y = wide("zw"), wide("gate"), wide("y")
+        pieces = [slice(k * PIECE, (k + 1) * PIECE) for k in range(I // PIECE)]
+        for cols in pieces:
+            nc.vector.scalar_tensor_tensor(zw[:, cols], p[:, cols], c[:], lean_ps[:, cols], ALU.mult, ALU.subtract)
+            nc.scalar.activation(gate[:, cols], zw[:, cols], ACT.Tanh, scale=tanh_scale[:])
+        for cols in pieces:
+            nc.vector.tensor_tensor(y[:, cols], gate[:, cols], base_t[:, cols], ALU.add)
+            if cols.stop % H == 0:
+                stored = slice(cols.stop - H, cols.stop)
+                nc.sync.dma_start(out=out[:, stored], in_=y[:, stored])

from contextlib import ExitStack

import concourse.mybir as mybir

D, T, I, Q = 512, 1024, 512, 128
FLOPS = 2 * D * T * Q

F32 = mybir.dt.float32
BF16 = mybir.dt.bfloat16
I32 = mybir.dt.int32
U32 = mybir.dt.uint32
U16 = mybir.dt.uint16
U8 = mybir.dt.uint8
FP8X4 = mybir.dt.float8_e4m3fn_x4
ALU = mybir.AluOpType
ACT = mybir.ActivationFunctionType

P = 128
PACK = 4
QUADRANTS = 4
PASS_WIDTHS = (256, 256, 256, 128, 128)
WORD_LOADS = 2
WORD_COLS = T // WORD_LOADS
HALVES = 2
PIECE = 128
H = I // HALVES
LIST_COLS = H // 16


def tile_attend_middle_leaning_gated_heads_kernel(
    tc, query, keys_words, keys_scales, lam, lean, base, gain2, offs, offs2, offs3, out
):
    nc = tc.nc
    with ExitStack() as ctx:
        sb = ctx.enter_context(tc.tile_pool(name="sb", bufs=1))
        psum = ctx.enter_context(tc.psum_pool(name="psum", bufs=1))

        q_raw = sb.tile([P, PACK, Q], F32, name="q_raw")
        nc.sync.dma_start(out=q_raw[:], in_=query.rearrange("(p j) q -> p j q", j=PACK))

        k_scales = sb.tile([P, T], U8, name="k_scales", align_bytes=64)
        for quad in range(QUADRANTS):
            (nc.sync if quad % 2 else nc.scalar).dma_start(
                out=k_scales[32 * quad : 32 * quad + 4, :].bitcast(I32),
                in_=keys_scales[0, 4 * quad : 4 * quad + 4, :].bitcast(I32),
            )
        words_in_hbm = keys_words[0].rearrange("p n t -> p (n t)").bitcast(I32)
        k_words = []
        for part in range(WORD_LOADS):
            words = sb.tile([P, WORD_COLS], U32, name="k_words%d" % part, align_bytes=64)
            nc.sync.dma_start(
                out=words[:].bitcast(I32), in_=words_in_hbm[:, part * WORD_COLS : (part + 1) * WORD_COLS]
            )
            k_words.append(words)

        lists = []
        for n, src in enumerate((offs, offs2, offs3)):
            lst = sb.tile([P, I // 16], U16, name="list%d" % n)
            nc.sync.dma_start(lst[:], src)
            lists.append(lst)

        lam_t = sb.tile([P, 1], F32, name="lam_t")
        lean_t = sb.tile([P, 1], F32, name="lean_t")
        gain_t = sb.tile([P, 1], F32, name="gain_t")
        base_t = sb.tile([P, I], F32, name="base_t")
        nc.sync.dma_start(out=lam_t[:], in_=lam)
        nc.sync.dma_start(out=lean_t[:], in_=lean)
        nc.sync.dma_start(out=gain_t[:], in_=gain2)
        nc.sync.dma_start(out=base_t[:], in_=base)

        neg_lam = sb.tile([P, 1], F32, name="neg_lam")
        nc.gpsimd.tensor_scalar(neg_lam[:], lam_t[:], -1.0, 0.0, ALU.mult, ALU.add)

        gain_128 = sb.tile([P, 1], F32, name="gain_128")
        nc.gpsimd.tensor_scalar(gain_128[:], gain_t[:], 128.0, 0.0, ALU.mult, ALU.add)

        q_bf = sb.tile([P, Q, PACK], BF16, name="q_bf", align_bytes=64)
        nc.vector.tensor_copy(out=q_bf[:], in_=q_raw[:].rearrange("p j q -> p q j"))
        q_words = sb.tile([P, Q], U32, name="q_words", align_bytes=64)
        q_scales = sb.tile([P, Q], U8, name="q_scales", align_bytes=64)
        nc.vector.quantize_mx(
            out=q_words[:].bitcast(FP8X4),
            scales=q_scales[:],
            in_=q_bf[:].rearrange("p q j -> p (q j)"),
        )

        a = sb.tile([P, T], F32, name="a")
        for n, width in enumerate(PASS_WIDTHS):
            begin = sum(PASS_WIDTHS[:n])
            cols = slice(begin, begin + width)
            part, at = divmod(begin, WORD_COLS)
            bank = psum.tile([P, width], F32, name="bank%d" % n)
            nc.tensor.matmul_mx(
                out=bank[:],
                lhsT=q_words[:].bitcast(FP8X4),
                lhsT_scale=q_scales[:],
                rhs=k_words[part][:, at : at + width].bitcast(FP8X4),
                rhs_scale=k_scales[:, cols],
                start=True,
                stop=True,
            )
            if n % 2 == 0:
                nc.vector.tensor_copy(out=a[:, cols], in_=bank[:])
            else:
                nc.scalar.copy(out=a[:, cols], in_=bank[:])

        def wide(name):
            return sb.tile([P, I], F32, name=name)

        def column(name):
            return sb.tile([P, 1], F32, name=name)

        def half(h):
            return slice(h * H, (h + 1) * H)

        def looked_up(n, h):
            return a[:].indirect(lists[n][:, h * LIST_COLS : (h + 1) * LIST_COLS])

        first, second, third = wide("first"), wide("second"), wide("third")
        for h in range(HALVES):
            nc.vector.tensor_copy(first[:, half(h)], looked_up(0, h))
            nc.scalar.activation(second[:, half(h)], looked_up(1, h), ACT.Copy)
        for h in range(HALVES):
            nc.scalar.activation(third[:, half(h)], looked_up(2, h), ACT.Copy)

        hi, lo, cap, mid, neg_s = wide("hi"), wide("lo"), wide("cap"), wide("mid"), wide("neg_s")
        for h in range(HALVES):
            nc.vector.tensor_tensor(hi[:, half(h)], first[:, half(h)], second[:, half(h)], ALU.max)
        nc.vector.tensor_tensor(lo[:], first[:], second[:], ALU.min)
        for h in range(HALVES):
            nc.vector.tensor_tensor(cap[:, half(h)], hi[:, half(h)], third[:, half(h)], ALU.min)
        for h in range(HALVES):
            nc.vector.tensor_tensor(mid[:, half(h)], lo[:, half(h)], cap[:, half(h)], ALU.max)
        neg_max = column("neg_max")
        nc.vector.tensor_scalar(neg_s[:], mid[:], neg_lam[:], None, ALU.mult, ALU.min, accum_out=neg_max[:])

        p, lean_ps = wide("p"), wide("lean_ps")
        p_sum = [column("p_sum%d" % h) for h in range(HALVES)]
        lean_sum = [column("lean_sum%d" % h) for h in range(HALVES)]
        for h in range(HALVES):
            nc.scalar.activation(
                p[:, half(h)], neg_s[:, half(h)], ACT.Exp, bias=neg_max[:], scale=-1.0, accum_out=p_sum[h][:]
            )
        for h in range(HALVES):
            nc.vector.scalar_tensor_tensor(
                lean_ps[:, half(h)],
                neg_s[:, half(h)],
                lean_t[:],
                p[:, half(h)],
                ALU.mult,
                ALU.mult,
                accum_out=lean_sum[h][:],
            )

        z, inv_z, partial, c, tanh_scale = (column(n) for n in ("z", "inv_z", "partial", "c", "tanh_scale"))
        nc.scalar.activation(z[:], p_sum[0][:], ACT.Identity, bias=p_sum[1][:])
        nc.vector.reciprocal(inv_z[:], z[:])
        nc.vector.tensor_scalar(partial[:], lean_sum[0][:], p_sum[0][:], p_sum[1][:], ALU.add, ALU.add)
        nc.vector.tensor_scalar(c[:], lean_sum[1][:], partial[:], inv_z[:], ALU.add, ALU.mult)
        nc.scalar.activation(tanh_scale[:], inv_z[:], ACT.Copy, scale=gain_128[:])

        zw, gate, y = wide("zw"), wide("gate"), wide("y")
        pieces = [slice(k * PIECE, (k + 1) * PIECE) for k in range(I // PIECE)]
        for cols in pieces:
            nc.vector.scalar_tensor_tensor(zw[:, cols], p[:, cols], c[:], lean_ps[:, cols], ALU.mult, ALU.subtract)
            nc.scalar.activation(gate[:, cols], zw[:, cols], ACT.Tanh, scale=tanh_scale[:])
        for cols in pieces:
            nc.vector.tensor_tensor(y[:, cols], gate[:, cols], base_t[:, cols], ALU.add)
            if cols.stop % H == 0:
                stored = slice(cols.stop - H, cols.stop)
                nc.sync.dma_start(out=out[:, stored], in_=y[:, stored])
